import numpy as np
import ml_dtypes


def mxq(x, axis, fmt="e4m3"):
    dtype, down = {"e4m3": (ml_dtypes.float8_e4m3fn, 7), "e5m2": (ml_dtypes.float8_e5m2, 14)}[fmt]
    v = np.moveaxis(np.asarray(x, np.float32).astype(ml_dtypes.bfloat16).astype(np.float64), axis, -1)
    blocks = v.reshape(v.shape[:-1] + (-1, 32))
    amax = np.abs(blocks).max(-1, keepdims=True)
    byte = np.maximum(np.where(amax > 0, np.frexp(amax)[1] - 1 + 127, 0) - down, 1)
    scale = np.exp2(byte - 127.0)
    codes = (blocks / scale).astype(np.float32).astype(dtype).astype(np.float64)
    return np.moveaxis((codes * scale).reshape(v.shape), -1, axis)


WIDE = False


def mx_kscale(k):
    if not WIDE:
        return np.ones(k)
    levels = np.array([10, -10, 5, -5, 0])
    if k % 512:
        return np.exp2(np.random.permutation(np.resize(levels, k // 32))).repeat(32)
    a = np.empty((k // 512, 16))
    for p in range(k // 512):
        a[p, :8] = np.random.permutation(np.resize(levels, 8))
        for g in range(8):
            far = levels[np.abs(levels - a[p, g]) >= 10]
            a[p, g + 8] = far[np.random.randint(len(far))]
    return np.exp2(a.ravel()).repeat(32)


def f64(x):
    return np.asarray(x).astype(np.float64)


def striped(idx):
    return np.tile(np.asarray(idx).reshape(-1, 16).T, (8, 1)).astype(np.uint16)


def unstriped(offs):
    return offs[:16].T.reshape(-1).astype(np.int64)


B, N, T, D, DV, NQ = 1, 512, 1024, 512, 0, 128
PAGE = 32
SEG = 32


def setup_inputs():
    n = np.random.standard_normal
    pages = np.random.permutation(T // PAGE)[:B * N // PAGE]
    idx = (pages[:, None] * PAGE + np.arange(PAGE)[None, :]).reshape(-1)
    s = mx_kscale(D)[:, None]
    return {
        "qT": (n((B, D, NQ)) * s * (1.00 / np.sqrt(D))).astype(np.float32),
        "kT": (n((D, T)) / s).astype(np.float32),
        "offs": striped(idx),
    }


def reference(qT, kT, offs):
    idx = unstriped(offs)
    pick = lambda x: x[:, idx].reshape(x.shape[0], B, N).transpose(1, 0, 2)
    a = mxq(f64(qT), 1, "e4m3").transpose(0, 2, 1) @ mxq(pick(f64(kT)), 1, "e4m3")
    return a.reshape(B, NQ, N // SEG, SEG).max(-1)

@@ -1,0 +1,101 @@
+from contextlib import ExitStack
+
+import concourse.mybir as mybir
+
+F32 = mybir.dt.float32
+BF16 = mybir.dt.bfloat16
+U32 = mybir.dt.uint32
+U16 = mybir.dt.uint16
+U8 = mybir.dt.uint8
+FP8X4 = mybir.dt.float8_e4m3fn_x4
+
+P = 128
+D, T, N, NQ, SEG = 512, 1024, 512, 128, 32
+PACK = 4
+FLOPS = 2 * D * N * NQ
+
+HALVES = 2
+W = N // HALVES
+OFFS_COLS = W // 16
+
+
+def tile_attend_maxsim_kernel(tc, qT, kT, offs, out):
+    nc = tc.nc
+    with ExitStack() as ctx:
+        keep = ctx.enter_context(tc.tile_pool(name="keep", bufs=1))
+        psum = ctx.enter_context(tc.psum_pool(name="psum", bufs=1))
+
+        k_rows = kT.rearrange("(p j) t -> p j t", j=PACK)
+        q_rows = qT[0].rearrange("(p j) q -> p j q", j=PACK)
+
+        lists = keep.tile([P, N // 16], U16, name="lists")
+        pairs = [keep.tile([P, T, 2], BF16, name=f"pairs{h}", align_bytes=64) for h in range(2)]
+        grouped = [keep.tile([P, W, PACK], BF16, name=f"grouped{i}", align_bytes=64) for i in range(HALVES)]
+        q_raw = keep.tile([P, PACK, NQ], F32, name="q_raw")
+        q_grouped = keep.tile([P, NQ, PACK], BF16, name="q_grouped", align_bytes=64)
+        q_codes = keep.tile([P, NQ], U32, name="q_codes", align_bytes=64)
+        q_scales = keep.tile([P, NQ], U8, name="q_scales", align_bytes=64)
+        result = keep.tile([P, N // SEG], F32, name="result")
+        dummy = keep.tile([P, 8], F32, name="dummy")
+
+        nc.vector.memset(dummy[:, 0:4], 0.0)
+        nc.scalar.copy(dummy[:, 4:8], dummy[:, 0:4])
+
+        chunks = [(0, 0, 512, "s"), (0, 512, 512, "v"), (1, 0, 512, "s"), (1, 512, 256, "s"), (1, 768, 256, "v")]
+        raws = []
+        for c, (h, t0, width, engine) in enumerate(chunks):
+            raw = keep.tile([P, 2, width], F32, name=f"raw{c}")
+            nc.sync.dma_start(out=raw[:], in_=k_rows[:, 2 * h : 2 * h + 2, t0 : t0 + width])
+            raws.append(raw)
+            if c == 1:
+                nc.sync.dma_start(lists[:], offs)
+        nc.sync.dma_start(out=q_raw[:], in_=q_rows)
+
+        for c, (h, t0, width, engine) in enumerate(chunks):
+            dst = pairs[h][:, t0 : t0 + width, :]
+            src = raws[c][:].rearrange("p j t -> p t j")
+            if engine == "s":
+                nc.scalar.copy(dst, src)
+            else:
+                nc.vector.tensor_copy(dst, src)
+            if (h, t0 + width) in ((0, T), (1, T)):
+                window = pairs[h][:].rearrange("p t j -> p (t j)").bitcast(U32)
+                for i in range(HALVES):
+                    words = grouped[i][:].rearrange("p n k -> p (n k)").bitcast(U32)
+                    words = words.rearrange("p (n h) -> p n h", h=2)
+                    nc.vector.tensor_copy(
+                        words[:, :, h], window.indirect(lists[:, i * OFFS_COLS : (i + 1) * OFFS_COLS])
+                    )
+
+        nc.scalar.copy(q_grouped[:], q_raw[:].rearrange("p j q -> p q j"))
+
+        def quantize(codes, scales, grouped_tile):
+            nc.vector.quantize_mx(
+                out=codes[:].bitcast(FP8X4), scales=scales[:], in_=grouped_tile[:].rearrange("p n k -> p (n k)")
+            )
+
+        quantize(q_codes, q_scales, q_grouped)
+        accs = []
+        for i in range(HALVES):
+            codes = keep.tile([P, W], U32, name=f"codes{i}", align_bytes=64)
+            scales = keep.tile([P, W], U8, name=f"scales{i}", align_bytes=64)
+            quantize(codes, scales, grouped[i])
+            acc = psum.tile([P, W], F32, name=f"acc{i}")
+            nc.tensor.matmul_mx(
+                out=acc[:],
+                lhsT=q_codes[:].bitcast(FP8X4),
+                lhsT_scale=q_scales[:],
+                rhs=codes[:].bitcast(FP8X4),
+                rhs_scale=scales[:],
+                start=True,
+                stop=True,
+            )
+            accs.append(acc)
+        for i in range(HALVES):
+            nc.vector.tensor_reduce(
+                out=result[:, i * W // SEG : (i + 1) * W // SEG],
+                in_=accs[i][:].rearrange("p (j s) -> p j s", s=SEG),
+                axis=mybir.AxisListType.X,
+                op=mybir.AluOpType.max,
+            )
+        nc.sync.dma_start(out=out[0], in_=result[:])

@@ -29,8 +29,12 @@ def tile_attend_maxsim_kernel(tc, qT, kT, offs, out):
         q_rows = qT[0].rearrange("(p j) q -> p j q", j=PACK)
 
         lists = keep.tile([P, N // 16], U16, name="lists")
-        pairs = [keep.tile([P, T, 2], BF16, name=f"pairs{h}", align_bytes=64) for h in range(2)]
+        planes = [keep.tile([P, T], F32, name=f"plane{j}") for j in range(PACK)]
+        picked = [keep.tile([P, 2, N], F32, name=f"picked{h}") for h in range(2)]
         grouped = [keep.tile([P, W, PACK], BF16, name=f"grouped{i}", align_bytes=64) for i in range(HALVES)]
+        codes = [keep.tile([P, W], U32, name=f"codes{i}", align_bytes=64) for i in range(HALVES)]
+        scales = [keep.tile([P, W], U8, name=f"scales{i}", align_bytes=64) for i in range(HALVES)]
+        accs = [psum.tile([P, W], F32, name=f"acc{i}") for i in range(HALVES)]
         q_raw = keep.tile([P, PACK, NQ], F32, name="q_raw")
         q_grouped = keep.tile([P, NQ, PACK], BF16, name="q_grouped", align_bytes=64)
         q_codes = keep.tile([P, NQ], U32, name="q_codes", align_bytes=64)
@@ -41,56 +45,51 @@ def tile_attend_maxsim_kernel(tc, qT, kT, offs, out):
         nc.vector.memset(dummy[:, 0:4], 0.0)
         nc.scalar.copy(dummy[:, 4:8], dummy[:, 0:4])
 
-        chunks = [(0, 0, 512, "s"), (0, 512, 512, "v"), (1, 0, 512, "s"), (1, 512, 256, "s"), (1, 768, 256, "v")]
-        raws = []
-        for c, (h, t0, width, engine) in enumerate(chunks):
-            raw = keep.tile([P, 2, width], F32, name=f"raw{c}")
-            nc.sync.dma_start(out=raw[:], in_=k_rows[:, 2 * h : 2 * h + 2, t0 : t0 + width])
-            raws.append(raw)
-            if c == 1:
+        for j in range(PACK):
+            nc.sync.dma_start(out=planes[j][:], in_=k_rows[:, j, :])
+            if j == 0:
                 nc.sync.dma_start(lists[:], offs)
         nc.sync.dma_start(out=q_raw[:], in_=q_rows)
 
-        for c, (h, t0, width, engine) in enumerate(chunks):
-            dst = pairs[h][:, t0 : t0 + width, :]
-            src = raws[c][:].rearrange("p j t -> p t j")
-            if engine == "s":
-                nc.scalar.copy(dst, src)
-            else:
-                nc.vector.tensor_copy(dst, src)
-            if (h, t0 + width) in ((0, T), (1, T)):
-                window = pairs[h][:].rearrange("p t j -> p (t j)").bitcast(U32)
-                for i in range(HALVES):
-                    words = grouped[i][:].rearrange("p n k -> p (n k)").bitcast(U32)
-                    words = words.rearrange("p (n h) -> p n h", h=2)
-                    nc.vector.tensor_copy(
-                        words[:, :, h], window.indirect(lists[:, i * OFFS_COLS : (i + 1) * OFFS_COLS])
-                    )
-
-        nc.scalar.copy(q_grouped[:], q_raw[:].rearrange("p j q -> p q j"))
-
-        def quantize(codes, scales, grouped_tile):
-            nc.vector.quantize_mx(
-                out=codes[:].bitcast(FP8X4), scales=scales[:], in_=grouped_tile[:].rearrange("p n k -> p (n k)")
+        def pair_into(copy, h, i):
+            copy(
+                grouped[i][:, :, 2 * h : 2 * h + 2],
+                picked[h][:, :, i * W : (i + 1) * W].rearrange("p j n -> p n j"),
             )
 
-        quantize(q_codes, q_scales, q_grouped)
-        accs = []
+        for j in range(PACK - 1):
+            nc.vector.tensor_copy(picked[j // 2][:, j % 2, :], planes[j][:].indirect(lists[:]))
         for i in range(HALVES):
-            codes = keep.tile([P, W], U32, name=f"codes{i}", align_bytes=64)
-            scales = keep.tile([P, W], U8, name=f"scales{i}", align_bytes=64)
-            quantize(codes, scales, grouped[i])
-            acc = psum.tile([P, W], F32, name=f"acc{i}")
+            pair_into(nc.scalar.copy, 0, i)
+        for i in range(HALVES):
+            nc.vector.tensor_copy(
+                picked[1][:, 1, i * W : (i + 1) * W],
+                planes[3][:].indirect(lists[:, i * OFFS_COLS : (i + 1) * OFFS_COLS]),
+            )
+        nc.scalar.copy(q_grouped[:], q_raw[:].rearrange("p j q -> p q j"))
+        for i in range(HALVES):
+            pair_into(nc.vector.tensor_copy, 1, i)
+
+        def quantize(codes_tile, scales_tile, grouped_tile):
+            nc.vector.quantize_mx(
+                out=codes_tile[:].bitcast(FP8X4),
+                scales=scales_tile[:],
+                in_=grouped_tile[:].rearrange("p n k -> p (n k)"),
+            )
+
+        quantize(codes[0], scales[0], grouped[0])
+        quantize(q_codes, q_scales, q_grouped)
+        quantize(codes[1], scales[1], grouped[1])
+        for i in range(HALVES):
             nc.tensor.matmul_mx(
-                out=acc[:],
+                out=accs[i][:],
                 lhsT=q_codes[:].bitcast(FP8X4),
                 lhsT_scale=q_scales[:],
-                rhs=codes[:].bitcast(FP8X4),
-                rhs_scale=scales[:],
+                rhs=codes[i][:].bitcast(FP8X4),
+                rhs_scale=scales[i][:],
                 start=True,
                 stop=True,
             )
-            accs.append(acc)
         for i in range(HALVES):
             nc.vector.tensor_reduce(
                 out=result[:, i * W // SEG : (i + 1) * W // SEG],

@@ -14,9 +14,7 @@ D, T, N, NQ, SEG = 512, 1024, 512, 128, 32
 PACK = 4
 FLOPS = 2 * D * N * NQ
 
-HALVES = 2
-W = N // HALVES
-OFFS_COLS = W // 16
+PIECES = ((0, 256), (256, 128), (384, 128))
 
 
 def tile_attend_maxsim_kernel(tc, qT, kT, offs, out):
@@ -31,10 +29,10 @@ def tile_attend_maxsim_kernel(tc, qT, kT, offs, out):
         lists = keep.tile([P, N // 16], U16, name="lists")
         planes = [keep.tile([P, T], F32, name=f"plane{j}") for j in range(PACK)]
         picked = [keep.tile([P, 2, N], F32, name=f"picked{h}") for h in range(2)]
-        grouped = [keep.tile([P, W, PACK], BF16, name=f"grouped{i}", align_bytes=64) for i in range(HALVES)]
-        codes = [keep.tile([P, W], U32, name=f"codes{i}", align_bytes=64) for i in range(HALVES)]
-        scales = [keep.tile([P, W], U8, name=f"scales{i}", align_bytes=64) for i in range(HALVES)]
-        accs = [psum.tile([P, W], F32, name=f"acc{i}") for i in range(HALVES)]
+        grouped = [keep.tile([P, w, PACK], BF16, name=f"grouped{i}", align_bytes=64) for i, (s, w) in enumerate(PIECES)]
+        codes = [keep.tile([P, w], U32, name=f"codes{i}", align_bytes=64) for i, (s, w) in enumerate(PIECES)]
+        scales = [keep.tile([P, w], U8, name=f"scales{i}", align_bytes=64) for i, (s, w) in enumerate(PIECES)]
+        accs = [psum.tile([P, w], F32, name=f"acc{i}") for i, (s, w) in enumerate(PIECES)]
         q_raw = keep.tile([P, PACK, NQ], F32, name="q_raw")
         q_grouped = keep.tile([P, NQ, PACK], BF16, name="q_grouped", align_bytes=64)
         q_codes = keep.tile([P, NQ], U32, name="q_codes", align_bytes=64)
@@ -52,23 +50,26 @@ def tile_attend_maxsim_kernel(tc, qT, kT, offs, out):
         nc.sync.dma_start(out=q_raw[:], in_=q_rows)
 
         def pair_into(copy, h, i):
-            copy(
-                grouped[i][:, :, 2 * h : 2 * h + 2],
-                picked[h][:, :, i * W : (i + 1) * W].rearrange("p j n -> p n j"),
+            s, w = PIECES[i]
+            copy(grouped[i][:, :, 2 * h : 2 * h + 2], picked[h][:, :, s : s + w].rearrange("p j n -> p n j"))
+
+        def gather(j, s, w):
+            nc.vector.tensor_copy(
+                picked[j // 2][:, j % 2, s : s + w], planes[j][:].indirect(lists[:, s // 16 : (s + w) // 16])
             )
 
-        for j in range(PACK - 1):
-            nc.vector.tensor_copy(picked[j // 2][:, j % 2, :], planes[j][:].indirect(lists[:]))
-        for i in range(HALVES):
-            pair_into(nc.scalar.copy, 0, i)
-        for i in range(HALVES):
-            nc.vector.tensor_copy(
-                picked[1][:, 1, i * W : (i + 1) * W],
-                planes[3][:].indirect(lists[:, i * OFFS_COLS : (i + 1) * OFFS_COLS]),
-            )
+        gather(0, 0, N)
+        gather(1, 0, N)
+        pair_into(nc.scalar.copy, 0, 0)
+        pair_into(nc.scalar.copy, 0, 1)
+        pair_into(nc.vector.tensor_copy, 0, 2)
+        gather(2, 0, N)
+        gather(3, 0, 256)
+        gather(3, 256, 256)
         nc.scalar.copy(q_grouped[:], q_raw[:].rearrange("p j q -> p q j"))
-        for i in range(HALVES):
-            pair_into(nc.vector.tensor_copy, 1, i)
+        pair_into(nc.vector.tensor_copy, 1, 0)
+        pair_into(nc.vector.tensor_copy, 1, 1)
+        pair_into(nc.scalar.copy, 1, 2)
 
         def quantize(codes_tile, scales_tile, grouped_tile):
             nc.vector.quantize_mx(
@@ -80,7 +81,8 @@ def tile_attend_maxsim_kernel(tc, qT, kT, offs, out):
         quantize(codes[0], scales[0], grouped[0])
         quantize(q_codes, q_scales, q_grouped)
         quantize(codes[1], scales[1], grouped[1])
-        for i in range(HALVES):
+        quantize(codes[2], scales[2], grouped[2])
+        for i in range(len(PIECES)):
             nc.tensor.matmul_mx(
                 out=accs[i][:],
                 lhsT=q_codes[:].bitcast(FP8X4),
@@ -90,9 +92,9 @@ def tile_attend_maxsim_kernel(tc, qT, kT, offs, out):
                 start=True,
                 stop=True,
             )
-        for i in range(HALVES):
+        for i, (s, w) in enumerate(PIECES):
             nc.vector.tensor_reduce(
-                out=result[:, i * W // SEG : (i + 1) * W // SEG],
+                out=result[:, s // SEG : (s + w) // SEG],
                 in_=accs[i][:].rearrange("p (j s) -> p j s", s=SEG),
                 axis=mybir.AxisListType.X,
                 op=mybir.AluOpType.max,

@@ -62,14 +62,14 @@ def tile_attend_maxsim_kernel(tc, qT, kT, offs, out):
         gather(1, 0, N)
         pair_into(nc.scalar.copy, 0, 0)
         pair_into(nc.scalar.copy, 0, 1)
-        pair_into(nc.vector.tensor_copy, 0, 2)
+        pair_into(nc.scalar.copy, 0, 2)
         gather(2, 0, N)
         gather(3, 0, 256)
         gather(3, 256, 256)
         nc.scalar.copy(q_grouped[:], q_raw[:].rearrange("p j q -> p q j"))
         pair_into(nc.vector.tensor_copy, 1, 0)
         pair_into(nc.vector.tensor_copy, 1, 1)
-        pair_into(nc.scalar.copy, 1, 2)
+        pair_into(nc.vector.tensor_copy, 1, 2)
 
         def quantize(codes_tile, scales_tile, grouped_tile):
             nc.vector.quantize_mx(

from contextlib import ExitStack

import concourse.mybir as mybir

F32 = mybir.dt.float32
BF16 = mybir.dt.bfloat16
U32 = mybir.dt.uint32
U16 = mybir.dt.uint16
U8 = mybir.dt.uint8
FP8X4 = mybir.dt.float8_e4m3fn_x4

P = 128
D, T, N, NQ, SEG = 512, 1024, 512, 128, 32
PACK = 4
FLOPS = 2 * D * N * NQ

PIECES = ((0, 256), (256, 128), (384, 128))


def tile_attend_maxsim_kernel(tc, qT, kT, offs, out):
    nc = tc.nc
    with ExitStack() as ctx:
        keep = ctx.enter_context(tc.tile_pool(name="keep", bufs=1))
        psum = ctx.enter_context(tc.psum_pool(name="psum", bufs=1))

        k_rows = kT.rearrange("(p j) t -> p j t", j=PACK)
        q_rows = qT[0].rearrange("(p j) q -> p j q", j=PACK)

        lists = keep.tile([P, N // 16], U16, name="lists")
        planes = [keep.tile([P, T], F32, name=f"plane{j}") for j in range(PACK)]
        picked = [keep.tile([P, 2, N], F32, name=f"picked{h}") for h in range(2)]
        grouped = [keep.tile([P, w, PACK], BF16, name=f"grouped{i}", align_bytes=64) for i, (s, w) in enumerate(PIECES)]
        codes = [keep.tile([P, w], U32, name=f"codes{i}", align_bytes=64) for i, (s, w) in enumerate(PIECES)]
        scales = [keep.tile([P, w], U8, name=f"scales{i}", align_bytes=64) for i, (s, w) in enumerate(PIECES)]
        accs = [psum.tile([P, w], F32, name=f"acc{i}") for i, (s, w) in enumerate(PIECES)]
        q_raw = keep.tile([P, PACK, NQ], F32, name="q_raw")
        q_grouped = keep.tile([P, NQ, PACK], BF16, name="q_grouped", align_bytes=64)
        q_codes = keep.tile([P, NQ], U32, name="q_codes", align_bytes=64)
        q_scales = keep.tile([P, NQ], U8, name="q_scales", align_bytes=64)
        result = keep.tile([P, N // SEG], F32, name="result")
        dummy = keep.tile([P, 8], F32, name="dummy")

        nc.vector.memset(dummy[:, 0:4], 0.0)
        nc.scalar.copy(dummy[:, 4:8], dummy[:, 0:4])

        for j in range(PACK):
            nc.sync.dma_start(out=planes[j][:], in_=k_rows[:, j, :])
            if j == 0:
                nc.sync.dma_start(lists[:], offs)
        nc.sync.dma_start(out=q_raw[:], in_=q_rows)

        def pair_into(copy, h, i):
            s, w = PIECES[i]
            copy(grouped[i][:, :, 2 * h : 2 * h + 2], picked[h][:, :, s : s + w].rearrange("p j n -> p n j"))

        def gather(j, s, w):
            nc.vector.tensor_copy(
                picked[j // 2][:, j % 2, s : s + w], planes[j][:].indirect(lists[:, s // 16 : (s + w) // 16])
            )

        gather(0, 0, N)
        gather(1, 0, N)
        pair_into(nc.scalar.copy, 0, 0)
        pair_into(nc.scalar.copy, 0, 1)
        pair_into(nc.scalar.copy, 0, 2)
        gather(2, 0, N)
        gather(3, 0, 256)
        gather(3, 256, 256)
        nc.scalar.copy(q_grouped[:], q_raw[:].rearrange("p j q -> p q j"))
        pair_into(nc.vector.tensor_copy, 1, 0)
        pair_into(nc.vector.tensor_copy, 1, 1)
        pair_into(nc.vector.tensor_copy, 1, 2)

        def quantize(codes_tile, scales_tile, grouped_tile):
            nc.vector.quantize_mx(
                out=codes_tile[:].bitcast(FP8X4),
                scales=scales_tile[:],
                in_=grouped_tile[:].rearrange("p n k -> p (n k)"),
            )

        quantize(codes[0], scales[0], grouped[0])
        quantize(q_codes, q_scales, q_grouped)
        quantize(codes[1], scales[1], grouped[1])
        quantize(codes[2], scales[2], grouped[2])
        for i in range(len(PIECES)):
            nc.tensor.matmul_mx(
                out=accs[i][:],
                lhsT=q_codes[:].bitcast(FP8X4),
                lhsT_scale=q_scales[:],
                rhs=codes[i][:].bitcast(FP8X4),
                rhs_scale=scales[i][:],
                start=True,
                stop=True,
            )
        for i, (s, w) in enumerate(PIECES):
            nc.vector.tensor_reduce(
                out=result[:, s // SEG : (s + w) // SEG],
                in_=accs[i][:].rearrange("p (j s) -> p j s", s=SEG),
                axis=mybir.AxisListType.X,
                op=mybir.AluOpType.max,
            )
        nc.sync.dma_start(out=out[0], in_=result[:])
